import numpy as np
import ml_dtypes


def mxq(x, axis, fmt="e4m3"):
    dtype, down = {"e4m3": (ml_dtypes.float8_e4m3fn, 7), "e5m2": (ml_dtypes.float8_e5m2, 14)}[fmt]
    v = np.moveaxis(np.asarray(x, np.float32).astype(ml_dtypes.bfloat16).astype(np.float64), axis, -1)
    blocks = v.reshape(v.shape[:-1] + (-1, 32))
    amax = np.abs(blocks).max(-1, keepdims=True)
    byte = np.maximum(np.where(amax > 0, np.frexp(amax)[1] - 1 + 127, 0) - down, 1)
    scale = np.exp2(byte - 127.0)
    codes = (blocks / scale).astype(np.float32).astype(dtype).astype(np.float64)
    return np.moveaxis((codes * scale).reshape(v.shape), -1, axis)


WIDE = False


def mx_kscale(k):
    if not WIDE:
        return np.ones(k)
    levels = np.array([10, -10, 5, -5, 0])
    if k % 512:
        return np.exp2(np.random.permutation(np.resize(levels, k // 32))).repeat(32)
    a = np.empty((k // 512, 16))
    for p in range(k // 512):
        a[p, :8] = np.random.permutation(np.resize(levels, 8))
        for g in range(8):
            far = levels[np.abs(levels - a[p, g]) >= 10]
            a[p, g + 8] = far[np.random.randint(len(far))]
    return np.exp2(a.ravel()).repeat(32)


def f64(x):
    return np.asarray(x).astype(np.float64)


def striped(idx):
    return np.tile(idx.reshape(-1, 16).T, (8, 1)).astype(np.uint16)


def unstriped(offs):
    return offs[:16].T.reshape(-1).astype(np.int64)


def pack_weight(w):
    k, n = w.shape
    w = f64(np.asarray(w, np.float32).astype(ml_dtypes.bfloat16)).reshape(k // 32, 32, n)
    amax = np.abs(w).max(1)
    byte = np.clip(np.where(amax > 0, np.frexp(amax)[1] - 1 + 127 - 7, 1), 1, 254)
    scaled = (w * np.exp2(127.0 - byte)[:, None, :]).reshape(k, n).astype(np.float32)
    words = np.ascontiguousarray(scaled.reshape(k // 512, 128, 4, n).transpose(0, 1, 3, 2)).astype(ml_dtypes.float8_e4m3fn).view(np.uint8)
    return words, np.ascontiguousarray(byte.astype(np.uint8).reshape(k // 512, 16, n))


def unpack_weight(words, scales):
    g, p, n, _ = words.shape
    vals = np.ascontiguousarray(words).view(ml_dtypes.float8_e4m3fn).astype(np.float64) * np.repeat(np.exp2(scales.astype(np.float64) - 127.0), 8, axis=1)[..., None]
    return vals.transpose(0, 1, 3, 2).reshape(g * 512, n)


def relu(v):
    return np.maximum(v, 0.0)


K, T, H, N = 512, 1024, 512, 128


def setup_inputs():
    n = np.random.standard_normal
    s = mx_kscale(K)[:, None]
    u = mx_kscale(H)
    packed_xT = pack_weight(n((K, T)) * s)
    packed_w2 = pack_weight(n((H, N)) / np.sqrt(2 * H) / u[:, None])
    packed_w3 = pack_weight(n((H, N)) / np.sqrt(2 * H) / u[:, None])
    return {
        "x_words": packed_xT[0],
        "x_scales": packed_xT[1],
        "w1": (n((K, H)) / np.sqrt(K) / s * u).astype(np.float32),
        "w2_words": packed_w2[0],
        "w2_scales": packed_w2[1],
        "w3_words": packed_w3[0],
        "w3_scales": packed_w3[1],
        "pos1": striped(np.random.permutation(T)),
        "pos2": striped(np.random.permutation(T)),
        "pos3": striped(np.random.permutation(T)),
    }


def reference(x_words, x_scales, w1, w2_words, w2_scales, w3_words, w3_scales, pos1, pos2, pos3):
    xq = unpack_weight(x_words, x_scales)
    h = relu(mxq(f64(w1), 0, "e4m3").T @ xq)
    z = (h[:, unstriped(pos1)] + h[:, unstriped(pos2)] + h[:, unstriped(pos3)]) / 3
    return unpack_weight(w2_words, w2_scales).T @ mxq(h, 0, "e4m3") + unpack_weight(w3_words, w3_scales).T @ mxq(z, 0, "e4m3")

@@ -1,0 +1,244 @@
+from contextlib import ExitStack
+
+import concourse.mybir as mybir
+from concourse.masks import make_identity
+
+K, T, H, N = 512, 1024, 512, 128
+FLOPS = 2 * K * H * T + 2 * 2 * H * N * T
+
+F32 = mybir.dt.float32
+BF16 = mybir.dt.bfloat16
+I32 = mybir.dt.int32
+U32 = mybir.dt.uint32
+U16 = mybir.dt.uint16
+U8 = mybir.dt.uint8
+FP8X4 = mybir.dt.float8_e4m3fn_x4
+ACT = mybir.ActivationFunctionType
+
+P = 128
+PACK = 4
+BANK = 512
+BLOCK = 128
+GATHER_CHUNKS = (640, 256, 128)
+OUT_CHUNKS = (512, 256, 128, 128)
+OUT_BANK = (3, 2, 4, 6)
+
+
+def tile_picked_wsagecat_mean_l_kernel(
+    tc, x_words, x_scales, w1, w2_words, w2_scales, w3_words, w3_scales, pos1, pos2, pos3, out
+):
+    nc = tc.nc
+    with ExitStack() as ctx:
+        keep = ctx.enter_context(tc.tile_pool(name="keep", bufs=1))
+        ring = ctx.enter_context(tc.tile_pool(name="ring", bufs=6))
+        psum = ctx.enter_context(tc.psum_pool(name="psum", bufs=1))
+        banks = [psum.tile([P, BANK], F32, name="bank%d" % b) for b in range(8)]
+
+        def load_scale_rows(queue, plane, rows):
+            for q in range(4):
+                queue.dma_start(
+                    out=plane[32 * q : 32 * q + 4, :].bitcast(I32), in_=rows[0, 4 * q : 4 * q + 4, :].bitcast(I32)
+                )
+
+        x_plane = keep.tile([P, T], U8, name="x_plane", align_bytes=64)
+        nc.gpsimd.memset(x_plane[:].bitcast(I32), 0)
+        w1_rows = w1.rearrange("(p j) c -> p j c", j=PACK)
+        w1_raw = []
+        x_rows = keep.tile([P, T], U8, name="x_rows")
+        for half in range(2):
+            raw = keep.tile([P, PACK, H // 2], F32, name="w1_raw%d" % half, align_bytes=64)
+            nc.sync.dma_start(out=raw[:], in_=w1_rows[:, :, half * (H // 2) : (half + 1) * (H // 2)])
+            w1_raw.append(raw)
+            if half == 0:
+                load_scale_rows(nc.sync, x_rows[:], x_scales)
+        x_bytes = x_words[0].rearrange("p n t -> p (n t)")
+        x_codes = []
+        for half in range(2):
+            codes = keep.tile([P, T // 2], U32, name="x_codes%d" % half, align_bytes=64)
+            nc.sync.dma_start(
+                out=codes[:].bitcast(I32), in_=x_bytes[:, half * 2 * T : (half + 1) * 2 * T].bitcast(I32)
+            )
+            x_codes.append(codes)
+        lists = []
+        for d, pos in enumerate((pos1, pos2, pos3)):
+            offsets = keep.tile([P, T // 16], U16, name="offsets%d" % d)
+            nc.sync.dma_start(offsets[:], pos)
+            lists.append(offsets)
+
+        identity = keep.tile([P, P], F32, name="identity")
+        make_identity(nc, identity[:])
+
+        for q in range(4):
+            rows = slice(32 * q, 32 * q + 4)
+            nc.vector.tensor_copy(out=x_plane[rows, :].bitcast(I32), in_=x_rows[rows, :].bitcast(I32))
+
+        w1_first = keep.tile([P, P, PACK], BF16, name="w1_first", align_bytes=64)
+        w1_rest = keep.tile([P, PACK - 1, P, PACK], BF16, name="w1_rest", align_bytes=64)
+        for half in range(2):
+            ms = slice(half * (P // 2), (half + 1) * (P // 2))
+            by_t = w1_raw[half][:].rearrange("p j (m t) -> p m j t", t=PACK)
+            nc.vector.tensor_copy(out=w1_first[:, ms, :], in_=by_t[:, :, :, 0])
+            nc.scalar.copy(out=w1_rest[:, :, ms, :].rearrange("p t m j -> p m j t"), in_=by_t[:, :, :, 1:])
+        w1_codes, w1_planes = [], []
+        for name, src_ap, count in (
+            ("a", w1_first[:].rearrange("p m j -> p (m j)"), 1),
+            ("b", w1_rest[:, 0, :, :].rearrange("p m j -> p (m j)"), 1),
+            ("c", w1_rest[:, 1:, :, :].rearrange("p t m j -> p (t m j)"), 2),
+        ):
+            codes = keep.tile([P, count * P], U32, name="w1_codes_" + name, align_bytes=64)
+            plane = keep.tile([P, count * P], U8, name="w1_plane_" + name, align_bytes=64)
+            nc.vector.quantize_mx(out=codes[:].bitcast(FP8X4), scales=plane[:], in_=src_ap)
+            for i in range(count):
+                w1_codes.append(codes[:, i * P : (i + 1) * P])
+                w1_planes.append(plane[:, i * P : (i + 1) * P])
+
+        last_words = keep.tile([P, 2 * N], U32, name="last_words", tag="w1_raw0", align_bytes=64)
+        last_plane = keep.tile([P, 2 * N], U8, name="last_plane", tag="w1_raw1", align_bytes=64)
+        nc.gpsimd.memset(last_plane[:].bitcast(I32), 0)
+        last_codes, last_planes = [], []
+        for a, (words, scales) in enumerate(((w2_words, w2_scales), (w3_words, w3_scales))):
+            codes = last_words[:, a * N : (a + 1) * N]
+            plane = last_plane[:, a * N : (a + 1) * N]
+            nc.sync.dma_start(out=codes.bitcast(I32), in_=words[0].rearrange("p n t -> p (n t)").bitcast(I32))
+            load_scale_rows(nc.sync, plane, scales)
+            last_codes.append(codes)
+            last_planes.append(plane)
+
+        h = keep.tile([P, PACK, T], F32, name="h")
+        pieces = [(0, q * 256, 256, q) for q in range(4)]
+        pieces = pieces + [(t, half * 512, 512, (2 + 2 * t + half) % 8) for t in range(1, PACK) for half in range(2)]
+        for t, n0, width, b in pieces:
+            half, c0 = divmod(n0, T // 2)
+            nc.tensor.matmul_mx(
+                out=banks[b][:, :width],
+                lhsT=w1_codes[t].bitcast(FP8X4),
+                lhsT_scale=w1_planes[t],
+                rhs=x_codes[half][:, c0 : c0 + width].bitcast(FP8X4),
+                rhs_scale=x_plane[:, n0 : n0 + width],
+                start=True,
+                stop=True,
+            )
+            if t == 0 and n0 % 512 == 256:
+                nc.vector.tensor_scalar_max(h[:, t, n0 : n0 + width], banks[b][:, :width], 0.0)
+            else:
+                nc.scalar.activation(h[:, t, n0 : n0 + width], banks[b][:, :width], ACT.Relu)
+
+        out_starts = [sum(OUT_CHUNKS[:c]) for c in range(len(OUT_CHUNKS))]
+        h_grouped, z_grouped = [], []
+        for c, width in enumerate(OUT_CHUNKS):
+            n0 = out_starts[c]
+            grouped = keep.tile([P, width, PACK], BF16, name="h_grouped%d" % c, align_bytes=64)
+            nc.scalar.copy(out=grouped[:], in_=h[:, :, n0 : n0 + width].rearrange("p t n -> p n t"))
+            h_grouped.append(grouped)
+            z_grouped.append(keep.tile([P, width, PACK], BF16, name="z_grouped%d" % c, align_bytes=64))
+
+        picked = {}
+        means = {}
+
+        def gather(c, t, tags):
+            g0, width = sum(GATHER_CHUNKS[:c]), GATHER_CHUNKS[c]
+            for d in range(3):
+                name = "picked%d_%d_%d" % (c, t, d)
+                if d in tags:
+                    tile = keep.tile([P, width], F32, name=name, tag=tags[d], align_bytes=64)
+                else:
+                    tile = ring.tile([P, width], F32, name=name, tag="picked", align_bytes=64)
+                nc.vector.tensor_copy(out=tile[:], in_=h[:, t, :].indirect(lists[d][:, g0 // 16 : (g0 + width) // 16]))
+                picked[(c, t, d)] = tile
+
+        def add_turned(c, t, block_banks):
+            for d in range(3):
+                for i, bank in enumerate(block_banks):
+                    nc.tensor.matmul(
+                        bank[:, t * P : (t + 1) * P],
+                        lhsT=picked[(c, t, d)][:, i * BLOCK : (i + 1) * BLOCK],
+                        rhs=identity[:],
+                        start=(d == 0),
+                        stop=(d == 2),
+                        is_transpose=True,
+                    )
+
+        def round_mean(blk, bank, u0, u1):
+            if u0 == 0:
+                means[blk] = keep.tile([BLOCK, 2, P, 2], BF16, name="mean%d" % blk)
+            nc.scalar.activation(
+                means[blk][:, u0:u1],
+                bank[:].rearrange("n (u e p) -> n u p e", u=2, e=2)[:, u0:u1],
+                ACT.Copy,
+                scale=1.0 / 3.0,
+            )
+
+        def turn_back(blk, back, u0, u1):
+            words = means[blk][:].rearrange("n u p e -> n (u p e)").bitcast(F32)
+            for u in range(u0, u1):
+                nc.tensor.transpose(back[:, u * BLOCK : (u + 1) * BLOCK], words[:, u * P : (u + 1) * P], identity[:])
+
+        def interleave(blk, back):
+            n0 = blk * BLOCK
+            c = max(i for i, s in enumerate(out_starts) if s <= n0)
+            c0 = n0 - out_starts[c]
+            dst = z_grouped[c][:, c0 : c0 + BLOCK, :].rearrange("p n t -> p (n t)").bitcast(F32)
+            nc.scalar.copy(out=dst.rearrange("p (n u) -> p n u", u=2), in_=back.rearrange("p (u n) -> p n u", u=2))
+
+        def product(c, a, codes):
+            width = OUT_CHUNKS[c]
+            grouped = (h_grouped, z_grouped)[a][c]
+            if codes is None:
+                codes = keep.tile([P, width], U32, name="codes%d_%d" % (a, c), align_bytes=64)
+            plane = keep.tile([P, width], U8, name="plane%d_%d" % (a, c), align_bytes=64)
+            nc.vector.quantize_mx(
+                out=codes[:].bitcast(FP8X4), scales=plane[:], in_=grouped[:].rearrange("p n t -> p (n t)")
+            )
+            nc.tensor.matmul_mx(
+                out=banks[OUT_BANK[c]][:, :width],
+                lhsT=last_codes[a].bitcast(FP8X4),
+                lhsT_scale=last_planes[a],
+                rhs=codes[:].bitcast(FP8X4),
+                rhs_scale=plane[:],
+                start=(a == 0),
+                stop=(a == 1),
+            )
+
+        def store(c):
+            n0, width = out_starts[c], OUT_CHUNKS[c]
+            result = keep.tile([P, width], F32, name="result%d" % c)
+            nc.scalar.copy(out=result[:], in_=banks[OUT_BANK[c]][:, :width])
+            nc.sync.dma_start(out=out[:, n0 : n0 + width], in_=result[:])
+
+        for t in range(PACK):
+            gather(0, t, {})
+            add_turned(0, t, banks[:5])
+        for blk in range(5):
+            round_mean(blk, banks[blk], 0, 2)
+            back = banks[5 + blk // 2][:, blk % 2 * 2 * BLOCK : (blk % 2 + 1) * 2 * BLOCK]
+            turn_back(blk, back, 0, 2)
+            interleave(blk, back)
+        product(0, 0, None)
+        for t in range(PACK - 1):
+            gather(1, t, {0: "h_grouped0"} if t == 0 else {})
+            add_turned(1, t, banks[:2])
+        product(0, 1, None)
+        store(0)
+        gather(1, 3, {0: "z_grouped0"})
+        add_turned(1, 3, banks[:2])
+        for i in range(2):
+            round_mean(5 + i, banks[i], 0, 2)
+            turn_back(5 + i, banks[5][:, i * 2 * BLOCK : (i + 1) * 2 * BLOCK], 0, 2)
+        for i in range(2):
+            interleave(5 + i, banks[5][:, i * 2 * BLOCK : (i + 1) * 2 * BLOCK])
+        for u in range(2):
+            for t in (2 * u, 2 * u + 1):
+                gather(2, t, {})
+                add_turned(2, t, [banks[u]])
+            round_mean(7, banks[u], u, u + 1)
+            turn_back(7, banks[7], u, u + 1)
+        interleave(7, banks[7][:, : 2 * BLOCK])
+        late = {}
+        for c, a in ((1, 1), (2, 1), (3, 1), (1, 0), (2, 0), (3, 0)):
+            late[(c, a)] = ring.tile(
+                [P, OUT_CHUNKS[c]], U32, name="codes%d_%d" % (a, c), tag="picked", align_bytes=64
+            )
+        for c in range(1, 4):
+            product(c, 0, late[(c, 0)])
+            product(c, 1, late.get((c, 1)))
+            store(c)

@@ -73,41 +73,29 @@ def tile_picked_wsagecat_mean_l_kernel(
             nc.vector.tensor_copy(out=x_plane[rows, :].bitcast(I32), in_=x_rows[rows, :].bitcast(I32))
 
         w1_first = keep.tile([P, P, PACK], BF16, name="w1_first", align_bytes=64)
-        w1_rest = keep.tile([P, PACK - 1, P, PACK], BF16, name="w1_rest", align_bytes=64)
+        w1_second = keep.tile([P, P, PACK], BF16, name="w1_second", align_bytes=64)
+        w1_rest = keep.tile([P, 2, P, PACK], BF16, name="w1_rest", align_bytes=64)
         for half in range(2):
             ms = slice(half * (P // 2), (half + 1) * (P // 2))
             by_t = w1_raw[half][:].rearrange("p j (m t) -> p m j t", t=PACK)
             nc.vector.tensor_copy(out=w1_first[:, ms, :], in_=by_t[:, :, :, 0])
-            nc.scalar.copy(out=w1_rest[:, :, ms, :].rearrange("p t m j -> p m j t"), in_=by_t[:, :, :, 1:])
+            if half == 0:
+                nc.scalar.copy(out=w1_second[:, ms, :], in_=by_t[:, :, :, 1])
+            nc.scalar.copy(out=w1_rest[:, :, ms, :].rearrange("p t m j -> p m j t"), in_=by_t[:, :, :, 2:])
         w1_codes, w1_planes = [], []
-        for name, src_ap, count in (
-            ("a", w1_first[:].rearrange("p m j -> p (m j)"), 1),
-            ("b", w1_rest[:, 0, :, :].rearrange("p m j -> p (m j)"), 1),
-            ("c", w1_rest[:, 1:, :, :].rearrange("p t m j -> p (t m j)"), 2),
-        ):
-            codes = keep.tile([P, count * P], U32, name="w1_codes_" + name, align_bytes=64)
+
+        def quantise_w1(name, src_ap, count, tag):
+            codes = keep.tile([P, count * P], U32, name="w1_codes_" + name, tag=tag, align_bytes=64)
             plane = keep.tile([P, count * P], U8, name="w1_plane_" + name, align_bytes=64)
             nc.vector.quantize_mx(out=codes[:].bitcast(FP8X4), scales=plane[:], in_=src_ap)
             for i in range(count):
                 w1_codes.append(codes[:, i * P : (i + 1) * P])
                 w1_planes.append(plane[:, i * P : (i + 1) * P])
 
-        last_words = keep.tile([P, 2 * N], U32, name="last_words", tag="w1_raw0", align_bytes=64)
-        last_plane = keep.tile([P, 2 * N], U8, name="last_plane", tag="w1_raw1", align_bytes=64)
-        nc.gpsimd.memset(last_plane[:].bitcast(I32), 0)
         last_codes, last_planes = [], []
-        for a, (words, scales) in enumerate(((w2_words, w2_scales), (w3_words, w3_scales))):
-            codes = last_words[:, a * N : (a + 1) * N]
-            plane = last_plane[:, a * N : (a + 1) * N]
-            nc.sync.dma_start(out=codes.bitcast(I32), in_=words[0].rearrange("p n t -> p (n t)").bitcast(I32))
-            load_scale_rows(nc.sync, plane, scales)
-            last_codes.append(codes)
-            last_planes.append(plane)
-
         h = keep.tile([P, PACK, T], F32, name="h")
-        pieces = [(0, q * 256, 256, q) for q in range(4)]
-        pieces = pieces + [(t, half * 512, 512, (2 + 2 * t + half) % 8) for t in range(1, PACK) for half in range(2)]
-        for t, n0, width, b in pieces:
+
+        def project(t, n0, width, b, on_vector):
             half, c0 = divmod(n0, T // 2)
             nc.tensor.matmul_mx(
                 out=banks[b][:, :width],
@@ -118,20 +106,13 @@ def tile_picked_wsagecat_mean_l_kernel(
                 start=True,
                 stop=True,
             )
-            if t == 0 and n0 % 512 == 256:
+            if on_vector:
                 nc.vector.tensor_scalar_max(h[:, t, n0 : n0 + width], banks[b][:, :width], 0.0)
             else:
                 nc.scalar.activation(h[:, t, n0 : n0 + width], banks[b][:, :width], ACT.Relu)
 
         out_starts = [sum(OUT_CHUNKS[:c]) for c in range(len(OUT_CHUNKS))]
         h_grouped, z_grouped = [], []
-        for c, width in enumerate(OUT_CHUNKS):
-            n0 = out_starts[c]
-            grouped = keep.tile([P, width, PACK], BF16, name="h_grouped%d" % c, align_bytes=64)
-            nc.scalar.copy(out=grouped[:], in_=h[:, :, n0 : n0 + width].rearrange("p t n -> p n t"))
-            h_grouped.append(grouped)
-            z_grouped.append(keep.tile([P, width, PACK], BF16, name="z_grouped%d" % c, align_bytes=64))
-
         picked = {}
         means = {}
 
@@ -139,11 +120,13 @@ def tile_picked_wsagecat_mean_l_kernel(
             g0, width = sum(GATHER_CHUNKS[:c]), GATHER_CHUNKS[c]
             for d in range(3):
                 name = "picked%d_%d_%d" % (c, t, d)
-                if d in tags:
-                    tile = keep.tile([P, width], F32, name=name, tag=tags[d], align_bytes=64)
+                if c == 2:
+                    tile = last_picked[:, 3 * t + d, :]
+                elif d in tags:
+                    tile = keep.tile([P, width], F32, name=name, tag=tags[d], align_bytes=64)[:]
                 else:
-                    tile = ring.tile([P, width], F32, name=name, tag="picked", align_bytes=64)
-                nc.vector.tensor_copy(out=tile[:], in_=h[:, t, :].indirect(lists[d][:, g0 // 16 : (g0 + width) // 16]))
+                    tile = ring.tile([P, width], F32, name=name, tag="picked", align_bytes=64)[:]
+                nc.vector.tensor_copy(out=tile, in_=h[:, t, :].indirect(lists[d][:, g0 // 16 : (g0 + width) // 16]))
                 picked[(c, t, d)] = tile
 
         def add_turned(c, t, block_banks):
@@ -184,16 +167,16 @@ def tile_picked_wsagecat_mean_l_kernel(
             width = OUT_CHUNKS[c]
             grouped = (h_grouped, z_grouped)[a][c]
             if codes is None:
-                codes = keep.tile([P, width], U32, name="codes%d_%d" % (a, c), align_bytes=64)
+                codes = keep.tile([P, width], U32, name="codes%d_%d" % (a, c), align_bytes=64)[:]
             plane = keep.tile([P, width], U8, name="plane%d_%d" % (a, c), align_bytes=64)
             nc.vector.quantize_mx(
-                out=codes[:].bitcast(FP8X4), scales=plane[:], in_=grouped[:].rearrange("p n t -> p (n t)")
+                out=codes.bitcast(FP8X4), scales=plane[:], in_=grouped[:].rearrange("p n t -> p (n t)")
             )
             nc.tensor.matmul_mx(
                 out=banks[OUT_BANK[c]][:, :width],
                 lhsT=last_codes[a].bitcast(FP8X4),
                 lhsT_scale=last_planes[a],
-                rhs=codes[:].bitcast(FP8X4),
+                rhs=codes.bitcast(FP8X4),
                 rhs_scale=plane[:],
                 start=(a == 0),
                 stop=(a == 1),
@@ -205,7 +188,37 @@ def tile_picked_wsagecat_mean_l_kernel(
             nc.scalar.copy(out=result[:], in_=banks[OUT_BANK[c]][:, :width])
             nc.sync.dma_start(out=out[:, n0 : n0 + width], in_=result[:])
 
-        for t in range(PACK):
+        quantise_w1("a", w1_first[:].rearrange("p m j -> p (m j)"), 1, "w1_codes_a")
+        nc.vector.tensor_copy(out=w1_second[:, P // 2 :, :], in_=by_t[:, :, :, 1])
+        last_words = keep.tile([P, 2 * N], U32, name="last_words", tag="w1_raw0", align_bytes=64)
+        last_plane = keep.tile([P, 2 * N], U8, name="last_plane", tag="w1_raw1", align_bytes=64)
+        nc.gpsimd.memset(last_plane[:].bitcast(I32), 0)
+        for a, (words, scales) in enumerate(((w2_words, w2_scales), (w3_words, w3_scales))):
+            codes = last_words[:, a * N : (a + 1) * N]
+            plane = last_plane[:, a * N : (a + 1) * N]
+            nc.sync.dma_start(out=codes.bitcast(I32), in_=words[0].rearrange("p n t -> p (n t)").bitcast(I32))
+            load_scale_rows(nc.sync, plane, scales)
+            last_codes.append(codes)
+            last_planes.append(plane)
+
+        for q in range(4):
+            project(0, q * 256, 256, q, q % 2 == 1)
+        quantise_w1("b", w1_second[:].rearrange("p m j -> p (m j)"), 1, "w1_codes_b")
+        gather(0, 0, {0: "first_picked"})
+        for half in range(2):
+            project(1, half * 512, 512, 2 + half, False)
+        add_turned(0, 0, banks[:5])
+        quantise_w1("c", w1_rest[:].rearrange("p t m j -> p (t m j)"), 2, "first_picked")
+        for i in range(4):
+            project(2 + i // 2, i % 2 * 512, 512, 5 + i % 3, False)
+        for c, width in enumerate(OUT_CHUNKS):
+            n0 = out_starts[c]
+            grouped = keep.tile([P, width, PACK], BF16, name="h_grouped%d" % c, align_bytes=64)
+            nc.scalar.copy(out=grouped[:], in_=h[:, :, n0 : n0 + width].rearrange("p t n -> p n t"))
+            h_grouped.append(grouped)
+            z_grouped.append(keep.tile([P, width, PACK], BF16, name="z_grouped%d" % c, align_bytes=64))
+
+        for t in range(1, PACK):
             gather(0, t, {})
             add_turned(0, t, banks[:5])
         for blk in range(5):
@@ -219,13 +232,14 @@ def tile_picked_wsagecat_mean_l_kernel(
             add_turned(1, t, banks[:2])
         product(0, 1, None)
         store(0)
-        gather(1, 3, {0: "z_grouped0"})
+        gather(1, 3, {})
         add_turned(1, 3, banks[:2])
         for i in range(2):
             round_mean(5 + i, banks[i], 0, 2)
             turn_back(5 + i, banks[5][:, i * 2 * BLOCK : (i + 1) * 2 * BLOCK], 0, 2)
         for i in range(2):
             interleave(5 + i, banks[5][:, i * 2 * BLOCK : (i + 1) * 2 * BLOCK])
+        last_picked = keep.tile([P, 3 * PACK, BLOCK], F32, name="last_picked", tag="z_grouped0", align_bytes=64)
         for u in range(2):
             for t in (2 * u, 2 * u + 1):
                 gather(2, t, {})
@@ -233,12 +247,9 @@ def tile_picked_wsagecat_mean_l_kernel(
             round_mean(7, banks[u], u, u + 1)
             turn_back(7, banks[7], u, u + 1)
         interleave(7, banks[7][:, : 2 * BLOCK])
-        late = {}
-        for c, a in ((1, 1), (2, 1), (3, 1), (1, 0), (2, 0), (3, 0)):
-            late[(c, a)] = ring.tile(
-                [P, OUT_CHUNKS[c]], U32, name="codes%d_%d" % (a, c), tag="picked", align_bytes=64
-            )
+        late = keep.tile([P, T // 2], U32, name="late_codes", tag="z_grouped0", align_bytes=64)
         for c in range(1, 4):
-            product(c, 0, late[(c, 0)])
-            product(c, 1, late.get((c, 1)))
+            c0 = out_starts[c] - T // 2
+            product(c, 0, late[:, c0 : c0 + OUT_CHUNKS[c]])
+            product(c, 1, None)
             store(c)

@@ -1,7 +1,6 @@
 from contextlib import ExitStack
 
 import concourse.mybir as mybir
-from concourse.masks import make_identity
 
 K, T, H, N = 512, 1024, 512, 128
 FLOPS = 2 * K * H * T + 2 * 2 * H * N * T
@@ -14,12 +13,13 @@ U16 = mybir.dt.uint16
 U8 = mybir.dt.uint8
 FP8X4 = mybir.dt.float8_e4m3fn_x4
 ACT = mybir.ActivationFunctionType
+ADD = mybir.AluOpType.add
 
 P = 128
 PACK = 4
 BANK = 512
 BLOCK = 128
-GATHER_CHUNKS = (640, 256, 128)
+GATHER_CHUNKS = (512, 384, 128)
 OUT_CHUNKS = (512, 256, 128, 128)
 OUT_BANK = (3, 2, 4, 6)
 
@@ -30,7 +30,6 @@ def tile_picked_wsagecat_mean_l_kernel(
     nc = tc.nc
     with ExitStack() as ctx:
         keep = ctx.enter_context(tc.tile_pool(name="keep", bufs=1))
-        ring = ctx.enter_context(tc.tile_pool(name="ring", bufs=6))
         psum = ctx.enter_context(tc.psum_pool(name="psum", bufs=1))
         banks = [psum.tile([P, BANK], F32, name="bank%d" % b) for b in range(8)]
 
@@ -65,8 +64,6 @@ def tile_picked_wsagecat_mean_l_kernel(
             nc.sync.dma_start(offsets[:], pos)
             lists.append(offsets)
 
-        identity = keep.tile([P, P], F32, name="identity")
-        make_identity(nc, identity[:])
 
         for q in range(4):
             rows = slice(32 * q, 32 * q + 4)
@@ -93,7 +90,7 @@ def tile_picked_wsagecat_mean_l_kernel(
                 w1_planes.append(plane[:, i * P : (i + 1) * P])
 
         last_codes, last_planes = [], []
-        h = keep.tile([P, PACK, T], F32, name="h")
+        h = [keep.tile([P, T], F32, name="h%d" % t) for t in range(PACK)]
 
         def project(t, n0, width, b, on_vector):
             half, c0 = divmod(n0, T // 2)
@@ -107,61 +104,36 @@ def tile_picked_wsagecat_mean_l_kernel(
                 stop=True,
             )
             if on_vector:
-                nc.vector.tensor_scalar_max(h[:, t, n0 : n0 + width], banks[b][:, :width], 0.0)
+                nc.vector.tensor_scalar_max(h[t][:, n0 : n0 + width], banks[b][:, :width], 0.0)
             else:
-                nc.scalar.activation(h[:, t, n0 : n0 + width], banks[b][:, :width], ACT.Relu)
+                nc.scalar.activation(h[t][:, n0 : n0 + width], banks[b][:, :width], ACT.Relu)
 
         out_starts = [sum(OUT_CHUNKS[:c]) for c in range(len(OUT_CHUNKS))]
         h_grouped, z_grouped = [], []
-        picked = {}
-        means = {}
+        sums = {}
 
-        def gather(c, t, tags):
+        def gather(c, ts, tags):
             g0, width = sum(GATHER_CHUNKS[:c]), GATHER_CHUNKS[c]
-            for d in range(3):
-                name = "picked%d_%d_%d" % (c, t, d)
-                if c == 2:
-                    tile = last_picked[:, 3 * t + d, :]
-                elif d in tags:
-                    tile = keep.tile([P, width], F32, name=name, tag=tags[d], align_bytes=64)[:]
-                else:
-                    tile = ring.tile([P, width], F32, name=name, tag="picked", align_bytes=64)[:]
-                nc.vector.tensor_copy(out=tile, in_=h[:, t, :].indirect(lists[d][:, g0 // 16 : (g0 + width) // 16]))
-                picked[(c, t, d)] = tile
+            cols = slice(g0 // 16, (g0 + width) // 16)
+            if ts[0] == 0:
+                sums[c] = keep.tile([P, PACK, width], F32, name="sums%d" % c)
+            one = keep.tile([P, 2, width], F32, name="one%d_%d" % (c, ts[0]), tag=tags[0], align_bytes=64)
+            two = keep.tile([P, 2, width], F32, name="two%d_%d" % (c, ts[0]), tag=tags[1], align_bytes=64)
+            for i, t in enumerate(ts):
+                nc.vector.tensor_copy(out=one[:, i, :], in_=h[t][:].indirect(lists[0][:, cols]))
+            for i, t in enumerate(ts):
+                nc.vector.tensor_tensor(two[:, i, :], h[t][:].indirect(lists[1][:, cols]), one[:, i, :], ADD)
+            for i, t in enumerate(ts):
+                nc.vector.tensor_tensor(sums[c][:, t, :], h[t][:].indirect(lists[2][:, cols]), two[:, i, :], ADD)
 
-        def add_turned(c, t, block_banks):
-            for d in range(3):
-                for i, bank in enumerate(block_banks):
-                    nc.tensor.matmul(
-                        bank[:, t * P : (t + 1) * P],
-                        lhsT=picked[(c, t, d)][:, i * BLOCK : (i + 1) * BLOCK],
-                        rhs=identity[:],
-                        start=(d == 0),
-                        stop=(d == 2),
-                        is_transpose=True,
-                    )
-
-        def round_mean(blk, bank, u0, u1):
-            if u0 == 0:
-                means[blk] = keep.tile([BLOCK, 2, P, 2], BF16, name="mean%d" % blk)
+        def interleave(c, g):
+            c0 = out_starts[c] - sum(GATHER_CHUNKS[:g])
             nc.scalar.activation(
-                means[blk][:, u0:u1],
-                bank[:].rearrange("n (u e p) -> n u p e", u=2, e=2)[:, u0:u1],
+                z_grouped[c][:],
+                sums[g][:, :, c0 : c0 + OUT_CHUNKS[c]].rearrange("p t n -> p n t"),
                 ACT.Copy,
                 scale=1.0 / 3.0,
             )
-
-        def turn_back(blk, back, u0, u1):
-            words = means[blk][:].rearrange("n u p e -> n (u p e)").bitcast(F32)
-            for u in range(u0, u1):
-                nc.tensor.transpose(back[:, u * BLOCK : (u + 1) * BLOCK], words[:, u * P : (u + 1) * P], identity[:])
-
-        def interleave(blk, back):
-            n0 = blk * BLOCK
-            c = max(i for i, s in enumerate(out_starts) if s <= n0)
-            c0 = n0 - out_starts[c]
-            dst = z_grouped[c][:, c0 : c0 + BLOCK, :].rearrange("p n t -> p (n t)").bitcast(F32)
-            nc.scalar.copy(out=dst.rearrange("p (n u) -> p n u", u=2), in_=back.rearrange("p (u n) -> p n u", u=2))
 
         def product(c, a, codes):
             width = OUT_CHUNKS[c]
@@ -204,50 +176,34 @@ def tile_picked_wsagecat_mean_l_kernel(
         for q in range(4):
             project(0, q * 256, 256, q, q % 2 == 1)
         quantise_w1("b", w1_second[:].rearrange("p m j -> p (m j)"), 1, "w1_codes_b")
-        gather(0, 0, {0: "first_picked"})
         for half in range(2):
-            project(1, half * 512, 512, 2 + half, False)
-        add_turned(0, 0, banks[:5])
-        quantise_w1("c", w1_rest[:].rearrange("p t m j -> p (t m j)"), 2, "first_picked")
+            project(1, half * 512, 512, 4 + half, False)
+        gather(0, (0, 1), ("one_a", "two_a"))
+        quantise_w1("c", w1_rest[:].rearrange("p t m j -> p (t m j)"), 2, "one_a")
         for i in range(4):
-            project(2 + i // 2, i % 2 * 512, 512, 5 + i % 3, False)
+            project(2 + i // 2, i % 2 * 512, 512, (6 + i) % 8, False)
+        h_rounded = keep.tile([P, PACK, T], BF16, name="h_rounded")
+        for t in range(PACK):
+            nc.scalar.copy(out=h_rounded[:, t, :], in_=h[t][:])
         for c, width in enumerate(OUT_CHUNKS):
             n0 = out_starts[c]
             grouped = keep.tile([P, width, PACK], BF16, name="h_grouped%d" % c, align_bytes=64)
-            nc.scalar.copy(out=grouped[:], in_=h[:, :, n0 : n0 + width].rearrange("p t n -> p n t"))
+            nc.scalar.copy(out=grouped[:], in_=h_rounded[:, :, n0 : n0 + width].rearrange("p t n -> p n t"))
             h_grouped.append(grouped)
             z_grouped.append(keep.tile([P, width, PACK], BF16, name="z_grouped%d" % c, align_bytes=64))
-
-        for t in range(1, PACK):
-            gather(0, t, {})
-            add_turned(0, t, banks[:5])
-        for blk in range(5):
-            round_mean(blk, banks[blk], 0, 2)
-            back = banks[5 + blk // 2][:, blk % 2 * 2 * BLOCK : (blk % 2 + 1) * 2 * BLOCK]
-            turn_back(blk, back, 0, 2)
-            interleave(blk, back)
+        gather(0, (2, 3), ("one_b", "two_b"))
+        interleave(0, 0)
+        gather(1, (0, 1), ("one_c", "two_a"))
+        gather(1, (2, 3), ("one_b", "two_b"))
         product(0, 0, None)
-        for t in range(PACK - 1):
-            gather(1, t, {0: "h_grouped0"} if t == 0 else {})
-            add_turned(1, t, banks[:2])
         product(0, 1, None)
         store(0)
-        gather(1, 3, {})
-        add_turned(1, 3, banks[:2])
-        for i in range(2):
-            round_mean(5 + i, banks[i], 0, 2)
-            turn_back(5 + i, banks[5][:, i * 2 * BLOCK : (i + 1) * 2 * BLOCK], 0, 2)
-        for i in range(2):
-            interleave(5 + i, banks[5][:, i * 2 * BLOCK : (i + 1) * 2 * BLOCK])
-        last_picked = keep.tile([P, 3 * PACK, BLOCK], F32, name="last_picked", tag="z_grouped0", align_bytes=64)
-        for u in range(2):
-            for t in (2 * u, 2 * u + 1):
-                gather(2, t, {})
-                add_turned(2, t, [banks[u]])
-            round_mean(7, banks[u], u, u + 1)
-            turn_back(7, banks[7], u, u + 1)
-        interleave(7, banks[7][:, : 2 * BLOCK])
-        late = keep.tile([P, T // 2], U32, name="late_codes", tag="z_grouped0", align_bytes=64)
+        interleave(1, 1)
+        interleave(2, 1)
+        gather(2, (0, 1), ("z_grouped0", "two_a"))
+        gather(2, (2, 3), ("h_grouped0", "two_b"))
+        interleave(3, 2)
+        late = keep.tile([P, T // 2], U32, name="late_codes", tag="two_b", align_bytes=64)
         for c in range(1, 4):
             c0 = out_starts[c] - T // 2
             product(c, 0, late[:, c0 : c0 + OUT_CHUNKS[c]])

@@ -17,85 +17,109 @@ ADD = mybir.AluOpType.add
 
 P = 128
 PACK = 4
+QUADRANTS = 4
 BANK = 512
-BLOCK = 128
-GATHER_CHUNKS = (512, 384, 128)
-OUT_CHUNKS = (512, 256, 128, 128)
-OUT_BANK = (3, 2, 4, 6)
+LIST_ROWS = 16
+FIRST_PIECE = 256
+LOOKUP_WIDTHS = (512, 384, 128)
+OUT_WIDTHS = (512, 256, 128, 128)
+STRETCH_OF_GROUP = (0, 1, 1, 2)
 
 
 def tile_picked_wsagecat_mean_l_kernel(
     tc, x_words, x_scales, w1, w2_words, w2_scales, w3_words, w3_scales, pos1, pos2, pos3, out
 ):
     nc = tc.nc
+    lookup_starts = [sum(LOOKUP_WIDTHS[:s]) for s in range(len(LOOKUP_WIDTHS))]
+    out_starts = [sum(OUT_WIDTHS[:g]) for g in range(len(OUT_WIDTHS))]
+    last_stretch, last_group = len(LOOKUP_WIDTHS) - 1, len(OUT_WIDTHS) - 1
+
     with ExitStack() as ctx:
         keep = ctx.enter_context(tc.tile_pool(name="keep", bufs=1))
         psum = ctx.enter_context(tc.psum_pool(name="psum", bufs=1))
-        banks = [psum.tile([P, BANK], F32, name="bank%d" % b) for b in range(8)]
+        h_banks = [psum.tile([P, BANK], F32, name="h_bank%d" % b) for b in range(T // FIRST_PIECE)]
+        out_banks = [psum.tile([P, BANK], F32, name="out_bank%d" % g) for g in range(len(OUT_WIDTHS))]
 
-        def load_scale_rows(queue, plane, rows):
-            for q in range(4):
-                queue.dma_start(
-                    out=plane[32 * q : 32 * q + 4, :].bitcast(I32), in_=rows[0, 4 * q : 4 * q + 4, :].bitcast(I32)
+        def load_scale_rows(plane, scales):
+            for q in range(QUADRANTS):
+                nc.sync.dma_start(
+                    out=plane[32 * q : 32 * q + 4, :].bitcast(I32), in_=scales[0, 4 * q : 4 * q + 4, :].bitcast(I32)
                 )
 
         x_plane = keep.tile([P, T], U8, name="x_plane", align_bytes=64)
         nc.gpsimd.memset(x_plane[:].bitcast(I32), 0)
+        x_scale_rows = keep.tile([P, T], U8, name="x_scale_rows")
         w1_rows = w1.rearrange("(p j) c -> p j c", j=PACK)
         w1_raw = []
-        x_rows = keep.tile([P, T], U8, name="x_rows")
         for half in range(2):
-            raw = keep.tile([P, PACK, H // 2], F32, name="w1_raw%d" % half, align_bytes=64)
-            nc.sync.dma_start(out=raw[:], in_=w1_rows[:, :, half * (H // 2) : (half + 1) * (H // 2)])
+            raw = keep.tile([P, 2, H], F32, name="w1_raw%d" % half, align_bytes=64)
+            nc.sync.dma_start(out=raw[:], in_=w1_rows[:, 2 * half : 2 * half + 2, :])
             w1_raw.append(raw)
             if half == 0:
-                load_scale_rows(nc.sync, x_rows[:], x_scales)
-        x_bytes = x_words[0].rearrange("p n t -> p (n t)")
+                load_scale_rows(x_scale_rows[:], x_scales)
+        x_bytes = x_words[0].rearrange("p n j -> p (n j)")
         x_codes = []
         for half in range(2):
-            codes = keep.tile([P, T // 2], U32, name="x_codes%d" % half, align_bytes=64)
+            codes = keep.tile([P, BANK], U32, name="x_codes%d" % half, align_bytes=64)
             nc.sync.dma_start(
-                out=codes[:].bitcast(I32), in_=x_bytes[:, half * 2 * T : (half + 1) * 2 * T].bitcast(I32)
+                out=codes[:].bitcast(I32),
+                in_=x_bytes[:, half * BANK * PACK : (half + 1) * BANK * PACK].bitcast(I32),
             )
             x_codes.append(codes)
         lists = []
         for d, pos in enumerate((pos1, pos2, pos3)):
-            offsets = keep.tile([P, T // 16], U16, name="offsets%d" % d)
+            offsets = keep.tile([P, T // LIST_ROWS], U16, name="offsets%d" % d)
             nc.sync.dma_start(offsets[:], pos)
             lists.append(offsets)
-
-
-        for q in range(4):
+        for q in range(QUADRANTS):
             rows = slice(32 * q, 32 * q + 4)
-            nc.vector.tensor_copy(out=x_plane[rows, :].bitcast(I32), in_=x_rows[rows, :].bitcast(I32))
+            nc.vector.tensor_copy(out=x_plane[rows, :].bitcast(I32), in_=x_scale_rows[rows, :].bitcast(I32))
 
-        w1_first = keep.tile([P, P, PACK], BF16, name="w1_first", align_bytes=64)
-        w1_second = keep.tile([P, P, PACK], BF16, name="w1_second", align_bytes=64)
-        w1_rest = keep.tile([P, 2, P, PACK], BF16, name="w1_rest", align_bytes=64)
+        w1_grouped0 = keep.tile([P, P, PACK], BF16, name="w1_grouped0", align_bytes=64)
+        w1_grouped1 = keep.tile([P, P, PACK], BF16, name="w1_grouped1", align_bytes=64)
+        w1_grouped23 = keep.tile([P, 2, P, PACK], BF16, name="w1_grouped23", align_bytes=64)
+        w1_by_t = [raw[:].rearrange("p e (m t) -> p m e t", t=PACK) for raw in w1_raw]
         for half in range(2):
-            ms = slice(half * (P // 2), (half + 1) * (P // 2))
-            by_t = w1_raw[half][:].rearrange("p j (m t) -> p m j t", t=PACK)
-            nc.vector.tensor_copy(out=w1_first[:, ms, :], in_=by_t[:, :, :, 0])
+            js = slice(2 * half, 2 * half + 2)
+            nc.vector.tensor_copy(out=w1_grouped0[:, :, js], in_=w1_by_t[half][:, :, :, 0])
             if half == 0:
-                nc.scalar.copy(out=w1_second[:, ms, :], in_=by_t[:, :, :, 1])
-            nc.scalar.copy(out=w1_rest[:, :, ms, :].rearrange("p t m j -> p m j t"), in_=by_t[:, :, :, 2:])
+                nc.scalar.copy(out=w1_grouped1[:, :, js], in_=w1_by_t[half][:, :, :, 1])
+            nc.scalar.copy(
+                out=w1_grouped23[:, :, :, js].rearrange("p t m e -> p m e t"), in_=w1_by_t[half][:, :, :, 2:]
+            )
+
         w1_codes, w1_planes = [], []
 
-        def quantise_w1(name, src_ap, count, tag):
-            codes = keep.tile([P, count * P], U32, name="w1_codes_" + name, tag=tag, align_bytes=64)
-            plane = keep.tile([P, count * P], U8, name="w1_plane_" + name, align_bytes=64)
-            nc.vector.quantize_mx(out=codes[:].bitcast(FP8X4), scales=plane[:], in_=src_ap)
-            for i in range(count):
+        def quantise_w1(grouped, tiles):
+            t = len(w1_codes)
+            codes = keep.tile([P, tiles * P], U32, name="w1_codes%d" % t, align_bytes=64)
+            plane = keep.tile([P, tiles * P], U8, name="w1_plane%d" % t, align_bytes=64)
+            nc.vector.quantize_mx(out=codes[:].bitcast(FP8X4), scales=plane[:], in_=grouped)
+            for i in range(tiles):
                 w1_codes.append(codes[:, i * P : (i + 1) * P])
                 w1_planes.append(plane[:, i * P : (i + 1) * P])
 
+        quantise_w1(w1_grouped0[:].rearrange("p m j -> p (m j)"), 1)
+        nc.vector.tensor_copy(out=w1_grouped1[:, :, 2:], in_=w1_by_t[1][:, :, :, 1])
+
+        last_words = keep.tile([P, 2 * N], U32, name="last_words", tag="w1_raw0", align_bytes=64)
+        last_bytes = keep.tile([P, 2 * N], U8, name="last_bytes", tag="w1_raw1", align_bytes=64)
+        nc.gpsimd.memset(last_bytes[:].bitcast(I32), 0)
         last_codes, last_planes = [], []
+        for a, (words, scales) in enumerate(((w2_words, w2_scales), (w3_words, w3_scales))):
+            codes = last_words[:, a * N : (a + 1) * N]
+            plane = last_bytes[:, a * N : (a + 1) * N]
+            nc.sync.dma_start(out=codes.bitcast(I32), in_=words[0].rearrange("p n j -> p (n j)").bitcast(I32))
+            load_scale_rows(plane, scales)
+            last_codes.append(codes)
+            last_planes.append(plane)
+
         h = [keep.tile([P, T], F32, name="h%d" % t) for t in range(PACK)]
 
-        def project(t, n0, width, b, on_vector):
-            half, c0 = divmod(n0, T // 2)
+        def project(t, n0, width, bank):
+            half, c0 = divmod(n0, BANK)
             nc.tensor.matmul_mx(
-                out=banks[b][:, :width],
+                out=bank[:, :width],
                 lhsT=w1_codes[t].bitcast(FP8X4),
                 lhsT_scale=w1_planes[t],
                 rhs=x_codes[half][:, c0 : c0 + width].bitcast(FP8X4),
@@ -103,109 +127,97 @@ def tile_picked_wsagecat_mean_l_kernel(
                 start=True,
                 stop=True,
             )
-            if on_vector:
-                nc.vector.tensor_scalar_max(h[t][:, n0 : n0 + width], banks[b][:, :width], 0.0)
-            else:
-                nc.scalar.activation(h[t][:, n0 : n0 + width], banks[b][:, :width], ACT.Relu)
+            nc.scalar.activation(h[t][:, n0 : n0 + width], bank[:, :width], ACT.Relu)
 
-        out_starts = [sum(OUT_CHUNKS[:c]) for c in range(len(OUT_CHUNKS))]
+        for piece, bank in enumerate(h_banks):
+            project(0, piece * FIRST_PIECE, FIRST_PIECE, bank)
+        quantise_w1(w1_grouped1[:].rearrange("p m j -> p (m j)"), 1)
+        quantise_w1(w1_grouped23[:].rearrange("p t m j -> p (t m j)"), 2)
+        for t in range(1, PACK):
+            for half, bank in enumerate(h_banks[-2:]):
+                project(t, half * BANK, BANK, bank)
+
+        h_rounded = keep.tile([P, PACK, T], BF16, name="h_rounded")
+        for t in range(PACK):
+            nc.scalar.copy(out=h_rounded[:, t, :], in_=h[t][:])
         h_grouped, z_grouped = [], []
-        sums = {}
+        for g, width in enumerate(OUT_WIDTHS):
+            grouped = keep.tile([P, width, PACK], BF16, name="h_grouped%d" % g, align_bytes=64)
+            nc.scalar.copy(
+                out=grouped[:], in_=h_rounded[:, :, out_starts[g] : out_starts[g] + width].rearrange("p t n -> p n t")
+            )
+            h_grouped.append(grouped)
+            z_grouped.append(keep.tile([P, width, PACK], BF16, name="z_grouped%d" % g, align_bytes=64))
 
-        def gather(c, ts, tags):
-            g0, width = sum(GATHER_CHUNKS[:c]), GATHER_CHUNKS[c]
-            cols = slice(g0 // 16, (g0 + width) // 16)
-            if ts[0] == 0:
-                sums[c] = keep.tile([P, PACK, width], F32, name="sums%d" % c)
-            one = keep.tile([P, 2, width], F32, name="one%d_%d" % (c, ts[0]), tag=tags[0], align_bytes=64)
-            two = keep.tile([P, 2, width], F32, name="two%d_%d" % (c, ts[0]), tag=tags[1], align_bytes=64)
-            for i, t in enumerate(ts):
-                nc.vector.tensor_copy(out=one[:, i, :], in_=h[t][:].indirect(lists[0][:, cols]))
-            for i, t in enumerate(ts):
-                nc.vector.tensor_tensor(two[:, i, :], h[t][:].indirect(lists[1][:, cols]), one[:, i, :], ADD)
-            for i, t in enumerate(ts):
-                nc.vector.tensor_tensor(sums[c][:, t, :], h[t][:].indirect(lists[2][:, cols]), two[:, i, :], ADD)
+        sums = [keep.tile([P, PACK, width], F32, name="sums%d" % s) for s, width in enumerate(LOOKUP_WIDTHS)]
 
-        def interleave(c, g):
-            c0 = out_starts[c] - sum(GATHER_CHUNKS[:g])
+        def look_up(jobs):
+            def neighbours(d, s, t):
+                c0 = lookup_starts[s] // LIST_ROWS
+                return h[t][:].indirect(lists[d][:, c0 : c0 + LOOKUP_WIDTHS[s] // LIST_ROWS])
+
+            for s, t, one, two in jobs:
+                nc.vector.tensor_copy(out=one, in_=neighbours(0, s, t))
+            for s, t, one, two in jobs:
+                nc.vector.tensor_tensor(two, neighbours(1, s, t), one, ADD)
+            for s, t, one, two in jobs:
+                nc.vector.tensor_tensor(sums[s][:, t, :], neighbours(2, s, t), two, ADD)
+
+        def job(s, t):
+            one = keep.tile([P, LOOKUP_WIDTHS[s]], F32, name="one%d_%d" % (s, t))
+            two = keep.tile([P, LOOKUP_WIDTHS[s]], F32, name="two%d_%d" % (s, t))
+            return s, t, one[:], two[:]
+
+        def round_mean(g):
+            s = STRETCH_OF_GROUP[g]
+            c0 = out_starts[g] - lookup_starts[s]
             nc.scalar.activation(
-                z_grouped[c][:],
-                sums[g][:, :, c0 : c0 + OUT_CHUNKS[c]].rearrange("p t n -> p n t"),
+                z_grouped[g][:],
+                sums[s][:, :, c0 : c0 + OUT_WIDTHS[g]].rearrange("p t n -> p n t"),
                 ACT.Copy,
                 scale=1.0 / 3.0,
             )
 
-        def product(c, a, codes):
-            width = OUT_CHUNKS[c]
-            grouped = (h_grouped, z_grouped)[a][c]
-            if codes is None:
-                codes = keep.tile([P, width], U32, name="codes%d_%d" % (a, c), align_bytes=64)[:]
-            plane = keep.tile([P, width], U8, name="plane%d_%d" % (a, c), align_bytes=64)
-            nc.vector.quantize_mx(
-                out=codes.bitcast(FP8X4), scales=plane[:], in_=grouped[:].rearrange("p n t -> p (n t)")
-            )
-            nc.tensor.matmul_mx(
-                out=banks[OUT_BANK[c]][:, :width],
-                lhsT=last_codes[a].bitcast(FP8X4),
-                lhsT_scale=last_planes[a],
-                rhs=codes.bitcast(FP8X4),
-                rhs_scale=plane[:],
-                start=(a == 0),
-                stop=(a == 1),
-            )
+        def finish(g, h_codes):
+            width = OUT_WIDTHS[g]
+            acc = out_banks[g][:, :width]
+            z_codes = keep.tile([P, width], U32, name="z_codes%d" % g, align_bytes=64)
+            for a, (grouped, codes) in enumerate(((h_grouped[g], h_codes), (z_grouped[g], z_codes[:]))):
+                plane = keep.tile([P, width], U8, name="plane%d_%d" % (a, g), align_bytes=64)
+                nc.vector.quantize_mx(
+                    out=codes.bitcast(FP8X4), scales=plane[:], in_=grouped[:].rearrange("p n t -> p (n t)")
+                )
+                nc.tensor.matmul_mx(
+                    out=acc,
+                    lhsT=last_codes[a].bitcast(FP8X4),
+                    lhsT_scale=last_planes[a],
+                    rhs=codes.bitcast(FP8X4),
+                    rhs_scale=plane[:],
+                    start=(a == 0),
+                    stop=(a == 1),
+                )
+            result = keep.tile([P, width], F32, name="result%d" % g)
+            if g == last_group:
+                nc.vector.tensor_copy(out=result[:], in_=acc)
+            else:
+                nc.scalar.copy(out=result[:], in_=acc)
+            nc.sync.dma_start(out=out[:, out_starts[g] : out_starts[g] + width], in_=result[:])
 
-        def store(c):
-            n0, width = out_starts[c], OUT_CHUNKS[c]
-            result = keep.tile([P, width], F32, name="result%d" % c)
-            nc.scalar.copy(out=result[:], in_=banks[OUT_BANK[c]][:, :width])
-            nc.sync.dma_start(out=out[:, n0 : n0 + width], in_=result[:])
+        order = [(0, 0), (1, 0)] + [(s, t) for s in range(last_stretch) for t in range(1, PACK)]
+        for i in range(0, len(order), 2):
+            look_up([job(s, t) for s, t in order[i : i + 2]])
+        for g in range(last_group):
+            round_mean(g)
+        h_codes0 = keep.tile([P, OUT_WIDTHS[0]], U32, name="h_codes0", align_bytes=64)
+        finish(0, h_codes0[:])
 
-        quantise_w1("a", w1_first[:].rearrange("p m j -> p (m j)"), 1, "w1_codes_a")
-        nc.vector.tensor_copy(out=w1_second[:, P // 2 :, :], in_=by_t[:, :, :, 1])
-        last_words = keep.tile([P, 2 * N], U32, name="last_words", tag="w1_raw0", align_bytes=64)
-        last_plane = keep.tile([P, 2 * N], U8, name="last_plane", tag="w1_raw1", align_bytes=64)
-        nc.gpsimd.memset(last_plane[:].bitcast(I32), 0)
-        for a, (words, scales) in enumerate(((w2_words, w2_scales), (w3_words, w3_scales))):
-            codes = last_words[:, a * N : (a + 1) * N]
-            plane = last_plane[:, a * N : (a + 1) * N]
-            nc.sync.dma_start(out=codes.bitcast(I32), in_=words[0].rearrange("p n t -> p (n t)").bitcast(I32))
-            load_scale_rows(nc.sync, plane, scales)
-            last_codes.append(codes)
-            last_planes.append(plane)
+        width = LOOKUP_WIDTHS[last_stretch]
+        ones = keep.tile([P, PACK, width], F32, name="ones", tag="z_grouped0", align_bytes=64)
+        twos = keep.tile([P, PACK, width], F32, name="twos", tag="h_grouped0", align_bytes=64)
+        look_up([(last_stretch, t, ones[:, t, :], twos[:, t, :]) for t in range(PACK)])
+        round_mean(last_group)
 
-        for q in range(4):
-            project(0, q * 256, 256, q, q % 2 == 1)
-        quantise_w1("b", w1_second[:].rearrange("p m j -> p (m j)"), 1, "w1_codes_b")
-        for half in range(2):
-            project(1, half * 512, 512, 4 + half, False)
-        gather(0, (0, 1), ("one_a", "two_a"))
-        quantise_w1("c", w1_rest[:].rearrange("p t m j -> p (t m j)"), 2, "one_a")
-        for i in range(4):
-            project(2 + i // 2, i % 2 * 512, 512, (6 + i) % 8, False)
-        h_rounded = keep.tile([P, PACK, T], BF16, name="h_rounded")
-        for t in range(PACK):
-            nc.scalar.copy(out=h_rounded[:, t, :], in_=h[t][:])
-        for c, width in enumerate(OUT_CHUNKS):
-            n0 = out_starts[c]
-            grouped = keep.tile([P, width, PACK], BF16, name="h_grouped%d" % c, align_bytes=64)
-            nc.scalar.copy(out=grouped[:], in_=h_rounded[:, :, n0 : n0 + width].rearrange("p t n -> p n t"))
-            h_grouped.append(grouped)
-            z_grouped.append(keep.tile([P, width, PACK], BF16, name="z_grouped%d" % c, align_bytes=64))
-        gather(0, (2, 3), ("one_b", "two_b"))
-        interleave(0, 0)
-        gather(1, (0, 1), ("one_c", "two_a"))
-        gather(1, (2, 3), ("one_b", "two_b"))
-        product(0, 0, None)
-        product(0, 1, None)
-        store(0)
-        interleave(1, 1)
-        interleave(2, 1)
-        gather(2, (0, 1), ("z_grouped0", "two_a"))
-        gather(2, (2, 3), ("h_grouped0", "two_b"))
-        interleave(3, 2)
-        late = keep.tile([P, T // 2], U32, name="late_codes", tag="two_b", align_bytes=64)
-        for c in range(1, 4):
-            c0 = out_starts[c] - T // 2
-            product(c, 0, late[:, c0 : c0 + OUT_CHUNKS[c]])
-            product(c, 1, None)
-            store(c)
+        late_codes = keep.tile([P, T - OUT_WIDTHS[0]], U32, name="late_codes", tag="h_grouped0", align_bytes=64)
+        for g in range(1, len(OUT_WIDTHS)):
+            c0 = out_starts[g] - OUT_WIDTHS[0]
+            finish(g, late_codes[:, c0 : c0 + OUT_WIDTHS[g]])

from contextlib import ExitStack

import concourse.mybir as mybir

K, T, H, N = 512, 1024, 512, 128
FLOPS = 2 * K * H * T + 2 * 2 * H * N * T

F32 = mybir.dt.float32
BF16 = mybir.dt.bfloat16
I32 = mybir.dt.int32
U32 = mybir.dt.uint32
U16 = mybir.dt.uint16
U8 = mybir.dt.uint8
FP8X4 = mybir.dt.float8_e4m3fn_x4
ACT = mybir.ActivationFunctionType
ADD = mybir.AluOpType.add

P = 128
PACK = 4
QUADRANTS = 4
BANK = 512
LIST_ROWS = 16
FIRST_PIECE = 256
LOOKUP_WIDTHS = (512, 384, 128)
OUT_WIDTHS = (512, 256, 128, 128)
STRETCH_OF_GROUP = (0, 1, 1, 2)


def tile_picked_wsagecat_mean_l_kernel(
    tc, x_words, x_scales, w1, w2_words, w2_scales, w3_words, w3_scales, pos1, pos2, pos3, out
):
    nc = tc.nc
    lookup_starts = [sum(LOOKUP_WIDTHS[:s]) for s in range(len(LOOKUP_WIDTHS))]
    out_starts = [sum(OUT_WIDTHS[:g]) for g in range(len(OUT_WIDTHS))]
    last_stretch, last_group = len(LOOKUP_WIDTHS) - 1, len(OUT_WIDTHS) - 1

    with ExitStack() as ctx:
        keep = ctx.enter_context(tc.tile_pool(name="keep", bufs=1))
        psum = ctx.enter_context(tc.psum_pool(name="psum", bufs=1))
        h_banks = [psum.tile([P, BANK], F32, name="h_bank%d" % b) for b in range(T // FIRST_PIECE)]
        out_banks = [psum.tile([P, BANK], F32, name="out_bank%d" % g) for g in range(len(OUT_WIDTHS))]

        def load_scale_rows(plane, scales):
            for q in range(QUADRANTS):
                nc.sync.dma_start(
                    out=plane[32 * q : 32 * q + 4, :].bitcast(I32), in_=scales[0, 4 * q : 4 * q + 4, :].bitcast(I32)
                )

        x_plane = keep.tile([P, T], U8, name="x_plane", align_bytes=64)
        nc.gpsimd.memset(x_plane[:].bitcast(I32), 0)
        x_scale_rows = keep.tile([P, T], U8, name="x_scale_rows")
        w1_rows = w1.rearrange("(p j) c -> p j c", j=PACK)
        w1_raw = []
        for half in range(2):
            raw = keep.tile([P, 2, H], F32, name="w1_raw%d" % half, align_bytes=64)
            nc.sync.dma_start(out=raw[:], in_=w1_rows[:, 2 * half : 2 * half + 2, :])
            w1_raw.append(raw)
            if half == 0:
                load_scale_rows(x_scale_rows[:], x_scales)
        x_bytes = x_words[0].rearrange("p n j -> p (n j)")
        x_codes = []
        for half in range(2):
            codes = keep.tile([P, BANK], U32, name="x_codes%d" % half, align_bytes=64)
            nc.sync.dma_start(
                out=codes[:].bitcast(I32),
                in_=x_bytes[:, half * BANK * PACK : (half + 1) * BANK * PACK].bitcast(I32),
            )
            x_codes.append(codes)
        lists = []
        for d, pos in enumerate((pos1, pos2, pos3)):
            offsets = keep.tile([P, T // LIST_ROWS], U16, name="offsets%d" % d)
            nc.sync.dma_start(offsets[:], pos)
            lists.append(offsets)
        for q in range(QUADRANTS):
            rows = slice(32 * q, 32 * q + 4)
            nc.vector.tensor_copy(out=x_plane[rows, :].bitcast(I32), in_=x_scale_rows[rows, :].bitcast(I32))

        w1_grouped0 = keep.tile([P, P, PACK], BF16, name="w1_grouped0", align_bytes=64)
        w1_grouped1 = keep.tile([P, P, PACK], BF16, name="w1_grouped1", align_bytes=64)
        w1_grouped23 = keep.tile([P, 2, P, PACK], BF16, name="w1_grouped23", align_bytes=64)
        w1_by_t = [raw[:].rearrange("p e (m t) -> p m e t", t=PACK) for raw in w1_raw]
        for half in range(2):
            js = slice(2 * half, 2 * half + 2)
            nc.vector.tensor_copy(out=w1_grouped0[:, :, js], in_=w1_by_t[half][:, :, :, 0])
            if half == 0:
                nc.scalar.copy(out=w1_grouped1[:, :, js], in_=w1_by_t[half][:, :, :, 1])
            nc.scalar.copy(
                out=w1_grouped23[:, :, :, js].rearrange("p t m e -> p m e t"), in_=w1_by_t[half][:, :, :, 2:]
            )

        w1_codes, w1_planes = [], []

        def quantise_w1(grouped, tiles):
            t = len(w1_codes)
            codes = keep.tile([P, tiles * P], U32, name="w1_codes%d" % t, align_bytes=64)
            plane = keep.tile([P, tiles * P], U8, name="w1_plane%d" % t, align_bytes=64)
            nc.vector.quantize_mx(out=codes[:].bitcast(FP8X4), scales=plane[:], in_=grouped)
            for i in range(tiles):
                w1_codes.append(codes[:, i * P : (i + 1) * P])
                w1_planes.append(plane[:, i * P : (i + 1) * P])

        quantise_w1(w1_grouped0[:].rearrange("p m j -> p (m j)"), 1)
        nc.vector.tensor_copy(out=w1_grouped1[:, :, 2:], in_=w1_by_t[1][:, :, :, 1])

        last_words = keep.tile([P, 2 * N], U32, name="last_words", tag="w1_raw0", align_bytes=64)
        last_bytes = keep.tile([P, 2 * N], U8, name="last_bytes", tag="w1_raw1", align_bytes=64)
        nc.gpsimd.memset(last_bytes[:].bitcast(I32), 0)
        last_codes, last_planes = [], []
        for a, (words, scales) in enumerate(((w2_words, w2_scales), (w3_words, w3_scales))):
            codes = last_words[:, a * N : (a + 1) * N]
            plane = last_bytes[:, a * N : (a + 1) * N]
            nc.sync.dma_start(out=codes.bitcast(I32), in_=words[0].rearrange("p n j -> p (n j)").bitcast(I32))
            load_scale_rows(plane, scales)
            last_codes.append(codes)
            last_planes.append(plane)

        h = [keep.tile([P, T], F32, name="h%d" % t) for t in range(PACK)]

        def project(t, n0, width, bank):
            half, c0 = divmod(n0, BANK)
            nc.tensor.matmul_mx(
                out=bank[:, :width],
                lhsT=w1_codes[t].bitcast(FP8X4),
                lhsT_scale=w1_planes[t],
                rhs=x_codes[half][:, c0 : c0 + width].bitcast(FP8X4),
                rhs_scale=x_plane[:, n0 : n0 + width],
                start=True,
                stop=True,
            )
            nc.scalar.activation(h[t][:, n0 : n0 + width], bank[:, :width], ACT.Relu)

        for piece, bank in enumerate(h_banks):
            project(0, piece * FIRST_PIECE, FIRST_PIECE, bank)
        quantise_w1(w1_grouped1[:].rearrange("p m j -> p (m j)"), 1)
        quantise_w1(w1_grouped23[:].rearrange("p t m j -> p (t m j)"), 2)
        for t in range(1, PACK):
            for half, bank in enumerate(h_banks[-2:]):
                project(t, half * BANK, BANK, bank)

        h_rounded = keep.tile([P, PACK, T], BF16, name="h_rounded")
        for t in range(PACK):
            nc.scalar.copy(out=h_rounded[:, t, :], in_=h[t][:])
        h_grouped, z_grouped = [], []
        for g, width in enumerate(OUT_WIDTHS):
            grouped = keep.tile([P, width, PACK], BF16, name="h_grouped%d" % g, align_bytes=64)
            nc.scalar.copy(
                out=grouped[:], in_=h_rounded[:, :, out_starts[g] : out_starts[g] + width].rearrange("p t n -> p n t")
            )
            h_grouped.append(grouped)
            z_grouped.append(keep.tile([P, width, PACK], BF16, name="z_grouped%d" % g, align_bytes=64))

        sums = [keep.tile([P, PACK, width], F32, name="sums%d" % s) for s, width in enumerate(LOOKUP_WIDTHS)]

        def look_up(jobs):
            def neighbours(d, s, t):
                c0 = lookup_starts[s] // LIST_ROWS
                return h[t][:].indirect(lists[d][:, c0 : c0 + LOOKUP_WIDTHS[s] // LIST_ROWS])

            for s, t, one, two in jobs:
                nc.vector.tensor_copy(out=one, in_=neighbours(0, s, t))
            for s, t, one, two in jobs:
                nc.vector.tensor_tensor(two, neighbours(1, s, t), one, ADD)
            for s, t, one, two in jobs:
                nc.vector.tensor_tensor(sums[s][:, t, :], neighbours(2, s, t), two, ADD)

        def job(s, t):
            one = keep.tile([P, LOOKUP_WIDTHS[s]], F32, name="one%d_%d" % (s, t))
            two = keep.tile([P, LOOKUP_WIDTHS[s]], F32, name="two%d_%d" % (s, t))
            return s, t, one[:], two[:]

        def round_mean(g):
            s = STRETCH_OF_GROUP[g]
            c0 = out_starts[g] - lookup_starts[s]
            nc.scalar.activation(
                z_grouped[g][:],
                sums[s][:, :, c0 : c0 + OUT_WIDTHS[g]].rearrange("p t n -> p n t"),
                ACT.Copy,
                scale=1.0 / 3.0,
            )

        def finish(g, h_codes):
            width = OUT_WIDTHS[g]
            acc = out_banks[g][:, :width]
            z_codes = keep.tile([P, width], U32, name="z_codes%d" % g, align_bytes=64)
            for a, (grouped, codes) in enumerate(((h_grouped[g], h_codes), (z_grouped[g], z_codes[:]))):
                plane = keep.tile([P, width], U8, name="plane%d_%d" % (a, g), align_bytes=64)
                nc.vector.quantize_mx(
                    out=codes.bitcast(FP8X4), scales=plane[:], in_=grouped[:].rearrange("p n t -> p (n t)")
                )
                nc.tensor.matmul_mx(
                    out=acc,
                    lhsT=last_codes[a].bitcast(FP8X4),
                    lhsT_scale=last_planes[a],
                    rhs=codes.bitcast(FP8X4),
                    rhs_scale=plane[:],
                    start=(a == 0),
                    stop=(a == 1),
                )
            result = keep.tile([P, width], F32, name="result%d" % g)
            if g == last_group:
                nc.vector.tensor_copy(out=result[:], in_=acc)
            else:
                nc.scalar.copy(out=result[:], in_=acc)
            nc.sync.dma_start(out=out[:, out_starts[g] : out_starts[g] + width], in_=result[:])

        order = [(0, 0), (1, 0)] + [(s, t) for s in range(last_stretch) for t in range(1, PACK)]
        for i in range(0, len(order), 2):
            look_up([job(s, t) for s, t in order[i : i + 2]])
        for g in range(last_group):
            round_mean(g)
        h_codes0 = keep.tile([P, OUT_WIDTHS[0]], U32, name="h_codes0", align_bytes=64)
        finish(0, h_codes0[:])

        width = LOOKUP_WIDTHS[last_stretch]
        ones = keep.tile([P, PACK, width], F32, name="ones", tag="z_grouped0", align_bytes=64)
        twos = keep.tile([P, PACK, width], F32, name="twos", tag="h_grouped0", align_bytes=64)
        look_up([(last_stretch, t, ones[:, t, :], twos[:, t, :]) for t in range(PACK)])
        round_mean(last_group)

        late_codes = keep.tile([P, T - OUT_WIDTHS[0]], U32, name="late_codes", tag="h_grouped0", align_bytes=64)
        for g in range(1, len(OUT_WIDTHS)):
            c0 = out_starts[g] - OUT_WIDTHS[0]
            finish(g, late_codes[:, c0 : c0 + OUT_WIDTHS[g]])
